import numpy as np
import ml_dtypes

BF16 = ml_dtypes.bfloat16


def bf(x):
    return np.asarray(x, np.float32).astype(BF16)


def f32(x):
    return np.asarray(x, np.float32)


def f64(x):
    return np.asarray(x).astype(np.float64)


def striped(idx):
    return np.tile(idx.reshape(-1, 16).T, (8, 1))


S, K, M, N = 2048, 128, 256, 2048


def setup_inputs():
    return {"table": bf(np.random.standard_normal((K, S))), "w": bf(np.random.standard_normal((K, M)) / np.sqrt(K)), "s": f32(0.5 + np.random.random_sample((M, 1))), "b": f32(0.5 * np.random.standard_normal((M, 1))), "offs": striped(np.random.permutation(S))}


def reference(table, w, s, b, offs):
    idx = offs[:16].T.reshape(-1)
    x = f64(table)[:, idx]
    y = f64(w).T @ x
    return y * f64(s) + f64(b)

@@ -1,0 +1,52 @@
+import concourse.mybir as mybir
+
+BF16, F32, U16 = mybir.dt.bfloat16, mybir.dt.float32, mybir.dt.uint16
+MULT, ADD = mybir.AluOpType.mult, mybir.AluOpType.add
+IDENTITY = mybir.ActivationFunctionType.Identity
+
+K, TOKENS, M, N = 128, 2048, 256, 2048
+P = 128
+PIECE = 512
+STRIPE = 16
+BLOCKS = M // P
+PIECES = N // PIECE
+FLOPS = 2 * K * M * N
+
+
+def tile_gather_matmul_kernel(tc, table, w, s, b, offs, out):
+    nc = tc.nc
+    with (
+        tc.tile_pool(name="held", bufs=1) as held,
+        tc.tile_pool(name="results", bufs=BLOCKS * PIECES) as results,
+        tc.psum_pool(name="psum", bufs=BLOCKS * PIECES) as psum,
+    ):
+        tokens = held.tile([K, TOKENS], BF16, name="tokens")
+        offsets = held.tile([P, N // STRIPE], U16, name="offsets")
+        weights = held.tile([K, M], BF16, name="weights")
+        gain = held.tile([P, BLOCKS], F32, name="gain")
+        shift = held.tile([P, BLOCKS], F32, name="shift")
+
+        nc.sync.dma_start(tokens[:], table)
+        nc.sync.dma_start(offsets[:], offs)
+        nc.scalar.dma_start(weights[:], w)
+        nc.scalar.dma_start(gain[:], s.rearrange("(i p) o -> p (i o)", p=P))
+        nc.scalar.dma_start(shift[:], b.rearrange("(i p) o -> p (i o)", p=P))
+
+        for q in range(PIECES):
+            columns = slice(q * PIECE, (q + 1) * PIECE)
+            piece = offsets[:, q * PIECE // STRIPE : (q + 1) * PIECE // STRIPE]
+            for i in range(BLOCKS):
+                features = slice(i * P, (i + 1) * P)
+                product = psum.tile([P, PIECE], F32, name="product")
+                nc.tensor.matmul(product[:], weights[:, features], tokens[:].indirect(piece), start=True, stop=True)
+
+                result = results.tile([P, PIECE], F32, name="result")
+                if i % 2 == 0:
+                    nc.vector.tensor_scalar(
+                        result[:], product[:], gain[:, i : i + 1], shift[:, i : i + 1], op0=MULT, op1=ADD
+                    )
+                else:
+                    nc.scalar.activation(
+                        result[:], product[:], IDENTITY, bias=shift[:, i : i + 1], scale=gain[:, i : i + 1]
+                    )
+                nc.sync.dma_start(out[features, columns], result[:])

@@ -29,8 +29,13 @@ def tile_gather_matmul_kernel(tc, table, w, s, b, offs, out):
         nc.sync.dma_start(tokens[:], table)
         nc.sync.dma_start(offsets[:], offs)
         nc.scalar.dma_start(weights[:], w)
-        nc.scalar.dma_start(gain[:], s.rearrange("(i p) o -> p (i o)", p=P))
-        nc.scalar.dma_start(shift[:], b.rearrange("(i p) o -> p (i o)", p=P))
+        nc.sync.dma_start(gain[:], s.rearrange("(i p) o -> p (i o)", p=P))
+        nc.sync.dma_start(shift[:], b.rearrange("(i p) o -> p (i o)", p=P))
+
+        zero = held.tile([P, 1], F32, name="zero")
+        primed = held.tile([P, 1], F32, name="primed")
+        nc.gpsimd.memset(zero[:], 0.0)
+        nc.scalar.activation(primed[:], zero[:], IDENTITY)
 
         for q in range(PIECES):
             columns = slice(q * PIECE, (q + 1) * PIECE)

@@ -29,21 +29,21 @@ def tile_gather_matmul_kernel(tc, table, w, s, b, offs, out):
         nc.sync.dma_start(tokens[:], table)
         nc.sync.dma_start(offsets[:], offs)
         nc.scalar.dma_start(weights[:], w)
-        nc.sync.dma_start(gain[:], s.rearrange("(i p) o -> p (i o)", p=P))
-        nc.sync.dma_start(shift[:], b.rearrange("(i p) o -> p (i o)", p=P))
+        nc.sync.dma_start(gain[:], s.rearrange("(p i) o -> p (i o)", i=BLOCKS))
+        nc.sync.dma_start(shift[:], b.rearrange("(p i) o -> p (i o)", i=BLOCKS))
 
         zero = held.tile([P, 1], F32, name="zero")
         primed = held.tile([P, 1], F32, name="primed")
         nc.gpsimd.memset(zero[:], 0.0)
         nc.scalar.activation(primed[:], zero[:], IDENTITY)
 
+        out_by_block = out.rearrange("(p i) n -> i p n", i=BLOCKS)
         for q in range(PIECES):
             columns = slice(q * PIECE, (q + 1) * PIECE)
             piece = offsets[:, q * PIECE // STRIPE : (q + 1) * PIECE // STRIPE]
             for i in range(BLOCKS):
-                features = slice(i * P, (i + 1) * P)
                 product = psum.tile([P, PIECE], F32, name="product")
-                nc.tensor.matmul(product[:], weights[:, features], tokens[:].indirect(piece), start=True, stop=True)
+                nc.tensor.matmul(product[:], weights[:, i::BLOCKS], tokens[:].indirect(piece), start=True, stop=True)
 
                 result = results.tile([P, PIECE], F32, name="result")
                 if i % 2 == 0:
@@ -54,4 +54,4 @@ def tile_gather_matmul_kernel(tc, table, w, s, b, offs, out):
                     nc.scalar.activation(
                         result[:], product[:], IDENTITY, bias=shift[:, i : i + 1], scale=gain[:, i : i + 1]
                     )
-                nc.sync.dma_start(out[features, columns], result[:])
+                nc.sync.dma_start(out_by_block[i, :, columns], result[:])

@@ -6,7 +6,8 @@ IDENTITY = mybir.ActivationFunctionType.Identity
 
 K, TOKENS, M, N = 128, 2048, 256, 2048
 P = 128
-PIECE = 512
+PIECE = 256
+BANKS = 8
 STRIPE = 16
 BLOCKS = M // P
 PIECES = N // PIECE
@@ -17,8 +18,8 @@ def tile_gather_matmul_kernel(tc, table, w, s, b, offs, out):
     nc = tc.nc
     with (
         tc.tile_pool(name="held", bufs=1) as held,
-        tc.tile_pool(name="results", bufs=BLOCKS * PIECES) as results,
-        tc.psum_pool(name="psum", bufs=BLOCKS * PIECES) as psum,
+        tc.tile_pool(name="results", bufs=PIECES) as results,
+        tc.psum_pool(name="psum", bufs=BANKS) as psum,
     ):
         tokens = held.tile([K, TOKENS], BF16, name="tokens")
         offsets = held.tile([P, N // STRIPE], U16, name="offsets")
@@ -37,21 +38,21 @@ def tile_gather_matmul_kernel(tc, table, w, s, b, offs, out):
         nc.gpsimd.memset(zero[:], 0.0)
         nc.scalar.activation(primed[:], zero[:], IDENTITY)
 
-        out_by_block = out.rearrange("(p i) n -> i p n", i=BLOCKS)
+        out_by_partition = out.rearrange("(p i) n -> p i n", i=BLOCKS)
         for q in range(PIECES):
             columns = slice(q * PIECE, (q + 1) * PIECE)
             piece = offsets[:, q * PIECE // STRIPE : (q + 1) * PIECE // STRIPE]
+            result = results.tile([P, BLOCKS, PIECE], F32, name="result")
             for i in range(BLOCKS):
                 product = psum.tile([P, PIECE], F32, name="product")
                 nc.tensor.matmul(product[:], weights[:, i::BLOCKS], tokens[:].indirect(piece), start=True, stop=True)
 
-                result = results.tile([P, PIECE], F32, name="result")
                 if i % 2 == 0:
                     nc.vector.tensor_scalar(
-                        result[:], product[:], gain[:, i : i + 1], shift[:, i : i + 1], op0=MULT, op1=ADD
+                        result[:, i, :], product[:], gain[:, i : i + 1], shift[:, i : i + 1], op0=MULT, op1=ADD
                     )
                 else:
                     nc.scalar.activation(
-                        result[:], product[:], IDENTITY, bias=shift[:, i : i + 1], scale=gain[:, i : i + 1]
+                        result[:, i, :], product[:], IDENTITY, bias=shift[:, i : i + 1], scale=gain[:, i : i + 1]
                     )
-                nc.sync.dma_start(out_by_block[i, :, columns], result[:])
+            nc.sync.dma_start(out_by_partition[:, :, columns], result[:])

import concourse.mybir as mybir

BF16, F32, U16 = mybir.dt.bfloat16, mybir.dt.float32, mybir.dt.uint16
MULT, ADD = mybir.AluOpType.mult, mybir.AluOpType.add
IDENTITY = mybir.ActivationFunctionType.Identity

K, TOKENS, M, N = 128, 2048, 256, 2048
P = 128
PIECE = 256
BANKS = 8
STRIPE = 16
BLOCKS = M // P
PIECES = N // PIECE
FLOPS = 2 * K * M * N


def tile_gather_matmul_kernel(tc, table, w, s, b, offs, out):
    nc = tc.nc
    with (
        tc.tile_pool(name="held", bufs=1) as held,
        tc.tile_pool(name="results", bufs=PIECES) as results,
        tc.psum_pool(name="psum", bufs=BANKS) as psum,
    ):
        tokens = held.tile([K, TOKENS], BF16, name="tokens")
        offsets = held.tile([P, N // STRIPE], U16, name="offsets")
        weights = held.tile([K, M], BF16, name="weights")
        gain = held.tile([P, BLOCKS], F32, name="gain")
        shift = held.tile([P, BLOCKS], F32, name="shift")

        nc.sync.dma_start(tokens[:], table)
        nc.sync.dma_start(offsets[:], offs)
        nc.scalar.dma_start(weights[:], w)
        nc.sync.dma_start(gain[:], s.rearrange("(p i) o -> p (i o)", i=BLOCKS))
        nc.sync.dma_start(shift[:], b.rearrange("(p i) o -> p (i o)", i=BLOCKS))

        zero = held.tile([P, 1], F32, name="zero")
        primed = held.tile([P, 1], F32, name="primed")
        nc.gpsimd.memset(zero[:], 0.0)
        nc.scalar.activation(primed[:], zero[:], IDENTITY)

        out_by_partition = out.rearrange("(p i) n -> p i n", i=BLOCKS)
        for q in range(PIECES):
            columns = slice(q * PIECE, (q + 1) * PIECE)
            piece = offsets[:, q * PIECE // STRIPE : (q + 1) * PIECE // STRIPE]
            result = results.tile([P, BLOCKS, PIECE], F32, name="result")
            for i in range(BLOCKS):
                product = psum.tile([P, PIECE], F32, name="product")
                nc.tensor.matmul(product[:], weights[:, i::BLOCKS], tokens[:].indirect(piece), start=True, stop=True)

                if i % 2 == 0:
                    nc.vector.tensor_scalar(
                        result[:, i, :], product[:], gain[:, i : i + 1], shift[:, i : i + 1], op0=MULT, op1=ADD
                    )
                else:
                    nc.scalar.activation(
                        result[:, i, :], product[:], IDENTITY, bias=shift[:, i : i + 1], scale=gain[:, i : i + 1]
                    )
            nc.sync.dma_start(out_by_partition[:, :, columns], result[:])
